import numpy as np
import ml_dtypes


def mxq(x, axis, fmt="e4m3"):
    dtype, down = {"e4m3": (ml_dtypes.float8_e4m3fn, 7), "e5m2": (ml_dtypes.float8_e5m2, 14)}[fmt]
    v = np.moveaxis(np.asarray(x, np.float32).astype(ml_dtypes.bfloat16).astype(np.float64), axis, -1)
    blocks = v.reshape(v.shape[:-1] + (-1, 32))
    amax = np.abs(blocks).max(-1, keepdims=True)
    byte = np.maximum(np.where(amax > 0, np.frexp(amax)[1] - 1 + 127, 0) - down, 1)
    scale = np.exp2(byte - 127.0)
    codes = (blocks / scale).astype(np.float32).astype(dtype).astype(np.float64)
    return np.moveaxis((codes * scale).reshape(v.shape), -1, axis)


WIDE = False


def mx_kscale(k):
    if not WIDE:
        return np.ones(k)
    levels = np.array([10, -10, 5, -5, 0])
    if k % 512:
        return np.exp2(np.random.permutation(np.resize(levels, k // 32))).repeat(32)
    a = np.empty((k // 512, 16))
    for p in range(k // 512):
        a[p, :8] = np.random.permutation(np.resize(levels, 8))
        for g in range(8):
            far = levels[np.abs(levels - a[p, g]) >= 10]
            a[p, g + 8] = far[np.random.randint(len(far))]
    return np.exp2(a.ravel()).repeat(32)


def f64(x):
    return np.asarray(x).astype(np.float64)


def striped(idx):
    return np.tile(idx.reshape(-1, 16).T, (8, 1)).astype(np.uint16)


def unstriped(offs):
    return offs[:16].T.reshape(-1).astype(np.int64)


K, T, E, C, N = 1536, 512, 8, 128, 512


def by_expert(wq, xq):
    return np.concatenate([wq[e].T @ xq[:, e * C:(e + 1) * C] for e in range(E)], axis=1)


def setup_inputs():
    n = np.random.standard_normal
    s = mx_kscale(K)[:, None]
    first = np.random.permutation(np.repeat(np.arange(E), T // E))
    second = (first + 1 + np.random.permutation(np.repeat(np.arange(E - 1), -(-T // (E - 1)))[:T])) % E
    while np.bincount(second, minlength=E).max() != T // E:
        load = np.bincount(second, minlength=E); hi, lo = int(load.argmax()), int(load.argmin())
        t = np.flatnonzero((second == hi) & (first != lo))[0]; second[t] = lo
    slot_token = np.empty(E * C, np.int64); pos = np.empty((2, T), np.int64); fill = np.zeros(E, np.int64)
    place = np.stack([np.random.permutation(C) for _ in range(E)])
    for r, deal in enumerate((first, second)):
        for t in np.random.permutation(T):
            e = deal[t]; j = e * C + place[e, fill[e]]; fill[e] += 1; slot_token[j] = t; pos[r, t] = j
    g = np.random.uniform(0.2, 0.8, T)
    return {
        "xT": (n((K, T)) * s).astype(np.float32),
        "w": (n((E, K, N)) / np.sqrt(K) / s[None]).astype(np.float32),
        "gate": np.stack([np.tile(g, (N, 1)), np.tile(1.0 - g, (N, 1))]).astype(np.float32),
        "offs": striped(slot_token),
        "pos1": striped(pos[0]),
        "pos2": striped(pos[1]),
    }


def reference(xT, w, gate, offs, pos1, pos2):
    idx = unstriped(offs)
    xq = mxq(f64(xT)[:, idx], 0, "e4m3")
    y = by_expert(mxq(f64(w), 1, "e4m3"), xq)
    return f64(gate[0]) * y[:, unstriped(pos1)] + f64(gate[1]) * y[:, unstriped(pos2)]

@@ -1,0 +1,146 @@
+from contextlib import ExitStack
+
+import concourse.mybir as mybir
+
+F32 = mybir.dt.float32
+BF16 = mybir.dt.bfloat16
+U32 = mybir.dt.uint32
+U16 = mybir.dt.uint16
+U8 = mybir.dt.uint8
+FP8X4 = mybir.dt.float8_e4m3fn_x4
+MULT = mybir.AluOpType.mult
+ADD = mybir.AluOpType.add
+
+K, T, E, C, N = 1536, 512, 8, 128, 512
+SLOTS = E * C
+FLOPS = 2 * K * SLOTS * N
+
+P = 128
+PACK = 4
+K_PASS = P * PACK
+PASSES = K // K_PASS
+BLOCKS = N // P
+BANK = 512
+LIST_COLUMN = 16
+GATHER_CUTS = ((0, 384), (384, 768), (768, 1024))
+
+PLAN = (
+    [(e, 0, 512) for e in range(6)]
+    + [("gate", 0), ("gate", 1), (6, 0, 256), (7, 0, 256), ("back", 0), ("back", 1)]
+    + [(6, 256, 256), (7, 256, 128), ("gate", 2), ("back", 2), (7, 384, 128), ("gate", 3), ("back", 3)]
+)
+VECTOR_TURNS = (9, 12, 15, 17, 19, 21, 23, 24, 26, 28, 30, 32)
+
+
+def interleave(copy, dst, src):
+    copy(
+        out=dst.rearrange("p (c i) t -> p c t i", i=4),
+        in_=src.rearrange("p t (c i) -> p c t i", i=4),
+    )
+
+
+def tile_routed_moe_kernel(tc, xT, w, gate, offs, pos1, pos2, out):
+    nc = tc.nc
+    with ExitStack() as ctx:
+        lists = ctx.enter_context(tc.tile_pool(name="lists", bufs=1))
+        keep = ctx.enter_context(tc.tile_pool(name="keep", bufs=1))
+        raw_pool = ctx.enter_context(tc.tile_pool(name="raw", bufs=13))
+        grouped_pool = ctx.enter_context(tc.tile_pool(name="grouped", bufs=6))
+        code_pool = ctx.enter_context(tc.tile_pool(name="codes", bufs=9))
+        stage = ctx.enter_context(tc.tile_pool(name="stage", bufs=2))
+        psum = ctx.enter_context(tc.psum_pool(name="psum", bufs=1))
+
+        offs_sb = lists.tile([P, SLOTS // LIST_COLUMN], U16, name="offs_sb")
+        pos1_sb = lists.tile([P, T // LIST_COLUMN], U16, name="pos1_sb")
+        pos2_sb = lists.tile([P, T // LIST_COLUMN], U16, name="pos2_sb")
+
+        token_words = [keep.tile([P, T], U32, name=f"token_words{a}", align_bytes=64) for a in range(PASSES)]
+        token_scales = [keep.tile([P, T], U8, name=f"token_scales{a}", align_bytes=64) for a in range(PASSES)]
+        slot_words = [keep.tile([P, SLOTS], U32, name=f"slot_words{a}", align_bytes=64) for a in range(PASSES)]
+        slot_scales = [keep.tile([P, SLOTS], U8, name=f"slot_scales{a}", align_bytes=64) for a in range(PASSES)]
+        for a in range(PASSES):
+            nc.gpsimd.memset(token_scales[a][:], 0)
+
+        for a in range(PASSES):
+            raw = raw_pool.tile([P, PACK, T], F32, name="raw")
+            nc.sync.dma_start(raw[:], xT[a * K_PASS : (a + 1) * K_PASS, :].rearrange("(p j) t -> p j t", j=PACK))
+            if a == 0:
+                nc.sync.dma_start(offs_sb[:], offs)
+            grouped = grouped_pool.tile([P, T, PACK], BF16, name="grouped", align_bytes=64)
+            interleave(nc.vector.tensor_copy if a % 2 == 0 else nc.scalar.copy, grouped[:], raw[:])
+            nc.vector.quantize_mx(
+                out=token_words[a][:].bitcast(FP8X4),
+                scales=token_scales[a][:],
+                in_=grouped[:].rearrange("p t j -> p (t j)"),
+            )
+        for j0, j1 in GATHER_CUTS:
+            for a in range(PASSES):
+                picked = offs_sb[:, j0 // LIST_COLUMN : j1 // LIST_COLUMN]
+                nc.vector.tensor_copy(slot_words[a][:, j0:j1], token_words[a][:].indirect(picked))
+                nc.vector.tensor_copy(slot_scales[a][:, j0:j1], token_scales[a][:].indirect(picked))
+        nc.sync.dma_start(pos1_sb[:], pos1)
+        nc.sync.dma_start(pos2_sb[:], pos2)
+
+        sums = [[psum.tile([P, BANK], F32, name=f"sums{b}_{h}") for h in range(2)] for b in range(BLOCKS)]
+        y = [keep.tile([P, SLOTS], F32, name=f"y{b}") for b in range(BLOCKS)]
+        gates = [keep.tile([P, 2, T], F32, name=f"gates{b}") for b in range(BLOCKS)]
+
+        def way_back(b):
+            first = stage.tile([P, T], F32, name="first")
+            second = stage.tile([P, T], F32, name="second")
+            total = stage.tile([P, T], F32, name="total")
+            nc.vector.tensor_tensor(first[:], y[b][:].indirect(pos1_sb[:]), gates[b][:, 0, :], MULT)
+            nc.vector.tensor_tensor(second[:], y[b][:].indirect(pos2_sb[:]), gates[b][:, 1, :], MULT)
+            nc.vector.tensor_tensor(total[:], first[:], second[:], ADD)
+            nc.sync.dma_start(out[b * P : (b + 1) * P, :], total[:])
+
+        turn = 0
+        for step in PLAN:
+            if step[0] == "gate":
+                b = step[1]
+                nc.sync.dma_start(gates[b][:], gate[:, b * P : (b + 1) * P, :].rearrange("g p t -> p g t"))
+                continue
+            if step[0] == "back":
+                way_back(step[1])
+                continue
+            e, n0, width = step
+            words = []
+            scales = []
+            for a in range(PASSES):
+                raw = raw_pool.tile([P, PACK, width], F32, name="raw")
+                nc.sync.dma_start(
+                    raw[:],
+                    w[e, a * K_PASS : (a + 1) * K_PASS, n0 : n0 + width].rearrange("(p j) n -> p j n", j=PACK),
+                )
+                grouped = grouped_pool.tile([P, width, PACK], BF16, name="grouped", align_bytes=64)
+                interleave(nc.vector.tensor_copy if turn in VECTOR_TURNS else nc.scalar.copy, grouped[:], raw[:])
+                turn += 1
+                w_words = code_pool.tile([P, width], U32, name="w_words", align_bytes=64)
+                w_scales = code_pool.tile([P, width], U8, name="w_scales", align_bytes=64)
+                nc.vector.quantize_mx(
+                    out=w_words[:].bitcast(FP8X4),
+                    scales=w_scales[:],
+                    in_=grouped[:].rearrange("p n j -> p (n j)"),
+                )
+                words.append(w_words)
+                scales.append(w_scales)
+            slots = slice(e * C, (e + 1) * C)
+            bank_slots = slice(e % 4 * C, (e % 4 + 1) * C)
+            for b in range(n0 // P, (n0 + width) // P):
+                cols = slice(b * P - n0, (b + 1) * P - n0)
+                for a in range(PASSES):
+                    nc.tensor.matmul_mx(
+                        out=sums[b][e // 4][:, bank_slots],
+                        lhsT=words[a][:, cols].bitcast(FP8X4),
+                        lhsT_scale=scales[a][:, cols],
+                        rhs=slot_words[a][:, slots].bitcast(FP8X4),
+                        rhs_scale=slot_scales[a][:, slots],
+                        start=(a == 0),
+                        stop=(a == PASSES - 1),
+                    )
+                if e == 3:
+                    nc.scalar.copy(out=y[b][:, 0:512], in_=sums[b][0][:])
+                elif e == 6:
+                    nc.scalar.copy(out=y[b][:, 512:896], in_=sums[b][1][:, 0:384])
+                elif e == 7:
+                    nc.scalar.copy(out=y[b][:, 896:1024], in_=sums[b][1][:, 384:512])

@@ -25,12 +25,15 @@ LIST_COLUMN = 16
 GATHER_CUTS = ((0, 384), (384, 768), (768, 1024))
 
 PLAN = (
-    [(e, 0, 512) for e in range(6)]
-    + [("gate", 0), ("gate", 1), (6, 0, 256), (7, 0, 256), ("back", 0), ("back", 1)]
-    + [(6, 256, 256), (7, 256, 128), ("gate", 2), ("back", 2), (7, 384, 128), ("gate", 3), ("back", 3)]
+    [(e, 0, 512) for e in range(3)]
+    + [(e, 0, 256) for e in range(3, 8)]
+    + [("gate", 0), ("gate", 1), ("back", 0), ("back", 1)]
+    + [(e, 256, 256) for e in range(3, 6)]
+    + [(e, 256, 128) for e in range(6, 8)]
+    + [("gate", 2), ("back", 2)]
+    + [(e, 384, 128) for e in range(6, 8)]
+    + [("gate", 3), ("back", 3)]
 )
-VECTOR_TURNS = (9, 12, 15, 17, 19, 21, 23, 24, 26, 28, 30, 32)
-
 
 def interleave(copy, dst, src):
     copy(
@@ -44,8 +47,8 @@ def tile_routed_moe_kernel(tc, xT, w, gate, offs, pos1, pos2, out):
     with ExitStack() as ctx:
         lists = ctx.enter_context(tc.tile_pool(name="lists", bufs=1))
         keep = ctx.enter_context(tc.tile_pool(name="keep", bufs=1))
-        raw_pool = ctx.enter_context(tc.tile_pool(name="raw", bufs=13))
-        grouped_pool = ctx.enter_context(tc.tile_pool(name="grouped", bufs=6))
+        raw_pool = ctx.enter_context(tc.tile_pool(name="raw", bufs=12))
+        grouped_pool = ctx.enter_context(tc.tile_pool(name="grouped", bufs=8))
         code_pool = ctx.enter_context(tc.tile_pool(name="codes", bufs=9))
         stage = ctx.enter_context(tc.tile_pool(name="stage", bufs=2))
         psum = ctx.enter_context(tc.psum_pool(name="psum", bufs=1))
@@ -67,7 +70,7 @@ def tile_routed_moe_kernel(tc, xT, w, gate, offs, pos1, pos2, out):
             if a == 0:
                 nc.sync.dma_start(offs_sb[:], offs)
             grouped = grouped_pool.tile([P, T, PACK], BF16, name="grouped", align_bytes=64)
-            interleave(nc.vector.tensor_copy if a % 2 == 0 else nc.scalar.copy, grouped[:], raw[:])
+            interleave(nc.vector.tensor_copy if a == 0 else nc.scalar.copy, grouped[:], raw[:])
             nc.vector.quantize_mx(
                 out=token_words[a][:].bitcast(FP8X4),
                 scales=token_scales[a][:],
@@ -92,9 +95,9 @@ def tile_routed_moe_kernel(tc, xT, w, gate, offs, pos1, pos2, out):
             nc.vector.tensor_tensor(first[:], y[b][:].indirect(pos1_sb[:]), gates[b][:, 0, :], MULT)
             nc.vector.tensor_tensor(second[:], y[b][:].indirect(pos2_sb[:]), gates[b][:, 1, :], MULT)
             nc.vector.tensor_tensor(total[:], first[:], second[:], ADD)
-            nc.sync.dma_start(out[b * P : (b + 1) * P, :], total[:])
+            queue = nc.sync if b == BLOCKS - 1 else nc.gpsimd
+            queue.dma_start(out[b * P : (b + 1) * P, :], total[:])
 
-        turn = 0
         for step in PLAN:
             if step[0] == "gate":
                 b = step[1]
@@ -113,8 +116,7 @@ def tile_routed_moe_kernel(tc, xT, w, gate, offs, pos1, pos2, out):
                     w[e, a * K_PASS : (a + 1) * K_PASS, n0 : n0 + width].rearrange("(p j) n -> p j n", j=PACK),
                 )
                 grouped = grouped_pool.tile([P, width, PACK], BF16, name="grouped", align_bytes=64)
-                interleave(nc.vector.tensor_copy if turn in VECTOR_TURNS else nc.scalar.copy, grouped[:], raw[:])
-                turn += 1
+                interleave(nc.vector.tensor_copy if a == PASSES - 1 else nc.scalar.copy, grouped[:], raw[:])
                 w_words = code_pool.tile([P, width], U32, name="w_words", align_bytes=64)
                 w_scales = code_pool.tile([P, width], U8, name="w_scales", align_bytes=64)
                 nc.vector.quantize_mx(

@@ -25,14 +25,12 @@ LIST_COLUMN = 16
 GATHER_CUTS = ((0, 384), (384, 768), (768, 1024))
 
 PLAN = (
-    [(e, 0, 512) for e in range(3)]
-    + [(e, 0, 256) for e in range(3, 8)]
-    + [("gate", 0), ("gate", 1), ("back", 0), ("back", 1)]
-    + [(e, 256, 256) for e in range(3, 6)]
-    + [(e, 256, 128) for e in range(6, 8)]
-    + [("gate", 2), ("back", 2)]
-    + [(e, 384, 128) for e in range(6, 8)]
-    + [("gate", 3), ("back", 3)]
+    [(e, 0, 512) for e in range(4)]
+    + [(e, 0, 256) for e in range(4, 8)]
+    + [("gate", 0), ("gate", 1)]
+    + [(e, 256, 256) for e in range(4, 8)]
+    + [("gate", 2), ("gate", 3)]
+    + [("back", b) for b in range(BLOCKS)]
 )
 
 def interleave(copy, dst, src):
@@ -47,7 +45,7 @@ def tile_routed_moe_kernel(tc, xT, w, gate, offs, pos1, pos2, out):
     with ExitStack() as ctx:
         lists = ctx.enter_context(tc.tile_pool(name="lists", bufs=1))
         keep = ctx.enter_context(tc.tile_pool(name="keep", bufs=1))
-        raw_pool = ctx.enter_context(tc.tile_pool(name="raw", bufs=12))
+        raw_pool = ctx.enter_context(tc.tile_pool(name="raw", bufs=14))
         grouped_pool = ctx.enter_context(tc.tile_pool(name="grouped", bufs=8))
         code_pool = ctx.enter_context(tc.tile_pool(name="codes", bufs=9))
         stage = ctx.enter_context(tc.tile_pool(name="stage", bufs=2))
@@ -58,49 +56,53 @@ def tile_routed_moe_kernel(tc, xT, w, gate, offs, pos1, pos2, out):
         pos2_sb = lists.tile([P, T // LIST_COLUMN], U16, name="pos2_sb")
 
         token_words = [keep.tile([P, T], U32, name=f"token_words{a}", align_bytes=64) for a in range(PASSES)]
-        token_scales = [keep.tile([P, T], U8, name=f"token_scales{a}", align_bytes=64) for a in range(PASSES)]
+        token_scales = keep.tile([P, T], U8, name="token_scales", align_bytes=64)
         slot_words = [keep.tile([P, SLOTS], U32, name=f"slot_words{a}", align_bytes=64) for a in range(PASSES)]
-        slot_scales = [keep.tile([P, SLOTS], U8, name=f"slot_scales{a}", align_bytes=64) for a in range(PASSES)]
-        for a in range(PASSES):
-            nc.gpsimd.memset(token_scales[a][:], 0)
+        slot_scales = keep.tile([P, SLOTS], U8, name="slot_scales", align_bytes=64)
+        nc.gpsimd.memset(token_scales[:], 0)
 
         for a in range(PASSES):
-            raw = raw_pool.tile([P, PACK, T], F32, name="raw")
+            raw = raw_pool.tile([P, PACK, T], F32, name="raw", tag="raw")
             nc.sync.dma_start(raw[:], xT[a * K_PASS : (a + 1) * K_PASS, :].rearrange("(p j) t -> p j t", j=PACK))
             if a == 0:
                 nc.sync.dma_start(offs_sb[:], offs)
             grouped = grouped_pool.tile([P, T, PACK], BF16, name="grouped", align_bytes=64)
-            interleave(nc.vector.tensor_copy if a == 0 else nc.scalar.copy, grouped[:], raw[:])
+            interleave(nc.scalar.copy if a == 1 else nc.vector.tensor_copy, grouped[:], raw[:])
             nc.vector.quantize_mx(
                 out=token_words[a][:].bitcast(FP8X4),
-                scales=token_scales[a][:],
+                scales=token_scales[4 * a : P, :],
                 in_=grouped[:].rearrange("p t j -> p (t j)"),
             )
         for j0, j1 in GATHER_CUTS:
+            picked = offs_sb[:, j0 // LIST_COLUMN : j1 // LIST_COLUMN]
             for a in range(PASSES):
-                picked = offs_sb[:, j0 // LIST_COLUMN : j1 // LIST_COLUMN]
                 nc.vector.tensor_copy(slot_words[a][:, j0:j1], token_words[a][:].indirect(picked))
-                nc.vector.tensor_copy(slot_scales[a][:, j0:j1], token_scales[a][:].indirect(picked))
+            nc.vector.tensor_copy(slot_scales[:, j0:j1], token_scales[:].indirect(picked))
         nc.sync.dma_start(pos1_sb[:], pos1)
         nc.sync.dma_start(pos2_sb[:], pos2)
 
         sums = [[psum.tile([P, BANK], F32, name=f"sums{b}_{h}") for h in range(2)] for b in range(BLOCKS)]
         y = [keep.tile([P, SLOTS], F32, name=f"y{b}") for b in range(BLOCKS)]
-        gates = [keep.tile([P, 2, T], F32, name=f"gates{b}") for b in range(BLOCKS)]
+        gates = {}
+        totals = keep.tile([P, BLOCKS, T], F32, name="totals")
 
         def way_back(b):
             first = stage.tile([P, T], F32, name="first")
             second = stage.tile([P, T], F32, name="second")
-            total = stage.tile([P, T], F32, name="total")
             nc.vector.tensor_tensor(first[:], y[b][:].indirect(pos1_sb[:]), gates[b][:, 0, :], MULT)
             nc.vector.tensor_tensor(second[:], y[b][:].indirect(pos2_sb[:]), gates[b][:, 1, :], MULT)
-            nc.vector.tensor_tensor(total[:], first[:], second[:], ADD)
-            queue = nc.sync if b == BLOCKS - 1 else nc.gpsimd
-            queue.dma_start(out[b * P : (b + 1) * P, :], total[:])
+            nc.vector.tensor_tensor(totals[:, b, :], first[:], second[:], ADD)
+            if b == BLOCKS - 2:
+                nc.sync.dma_start(
+                    out[0 : (b + 1) * P, :].rearrange("(b p) t -> p b t", p=P), totals[:, 0 : b + 1, :]
+                )
+            elif b == BLOCKS - 1:
+                nc.sync.dma_start(out[b * P : (b + 1) * P, :], totals[:, b, :])
 
         for step in PLAN:
             if step[0] == "gate":
                 b = step[1]
+                gates[b] = raw_pool.tile([P, 2, T], F32, name="gates", tag="raw")
                 nc.sync.dma_start(gates[b][:], gate[:, b * P : (b + 1) * P, :].rearrange("g p t -> p g t"))
                 continue
             if step[0] == "back":
@@ -110,7 +112,7 @@ def tile_routed_moe_kernel(tc, xT, w, gate, offs, pos1, pos2, out):
             words = []
             scales = []
             for a in range(PASSES):
-                raw = raw_pool.tile([P, PACK, width], F32, name="raw")
+                raw = raw_pool.tile([P, PACK, width], F32, name="raw", tag="raw")
                 nc.sync.dma_start(
                     raw[:],
                     w[e, a * K_PASS : (a + 1) * K_PASS, n0 : n0 + width].rearrange("(p j) n -> p j n", j=PACK),
@@ -136,7 +138,7 @@ def tile_routed_moe_kernel(tc, xT, w, gate, offs, pos1, pos2, out):
                         lhsT=words[a][:, cols].bitcast(FP8X4),
                         lhsT_scale=scales[a][:, cols],
                         rhs=slot_words[a][:, slots].bitcast(FP8X4),
-                        rhs_scale=slot_scales[a][:, slots],
+                        rhs_scale=slot_scales[4 * a : P, slots],
                         start=(a == 0),
                         stop=(a == PASSES - 1),
                     )

@@ -27,10 +27,9 @@ GATHER_CUTS = ((0, 384), (384, 768), (768, 1024))
 PLAN = (
     [(e, 0, 512) for e in range(4)]
     + [(e, 0, 256) for e in range(4, 8)]
-    + [("gate", 0), ("gate", 1)]
+    + [("gate", 0), ("gate", 1), ("back", 0)]
     + [(e, 256, 256) for e in range(4, 8)]
-    + [("gate", 2), ("gate", 3)]
-    + [("back", b) for b in range(BLOCKS)]
+    + [("gate", 2), ("gate", 3), ("back", 2)]
 )
 
 def interleave(copy, dst, src):
@@ -45,7 +44,7 @@ def tile_routed_moe_kernel(tc, xT, w, gate, offs, pos1, pos2, out):
     with ExitStack() as ctx:
         lists = ctx.enter_context(tc.tile_pool(name="lists", bufs=1))
         keep = ctx.enter_context(tc.tile_pool(name="keep", bufs=1))
-        raw_pool = ctx.enter_context(tc.tile_pool(name="raw", bufs=14))
+        raw_pool = ctx.enter_context(tc.tile_pool(name="raw", bufs=13))
         grouped_pool = ctx.enter_context(tc.tile_pool(name="grouped", bufs=8))
         code_pool = ctx.enter_context(tc.tile_pool(name="codes", bufs=9))
         stage = ctx.enter_context(tc.tile_pool(name="stage", bufs=2))
@@ -56,10 +55,11 @@ def tile_routed_moe_kernel(tc, xT, w, gate, offs, pos1, pos2, out):
         pos2_sb = lists.tile([P, T // LIST_COLUMN], U16, name="pos2_sb")
 
         token_words = [keep.tile([P, T], U32, name=f"token_words{a}", align_bytes=64) for a in range(PASSES)]
-        token_scales = keep.tile([P, T], U8, name="token_scales", align_bytes=64)
+        token_scales = [keep.tile([P, T], U8, name=f"token_scales{a}", align_bytes=64) for a in range(PASSES)]
         slot_words = [keep.tile([P, SLOTS], U32, name=f"slot_words{a}", align_bytes=64) for a in range(PASSES)]
-        slot_scales = keep.tile([P, SLOTS], U8, name="slot_scales", align_bytes=64)
-        nc.gpsimd.memset(token_scales[:], 0)
+        slot_scales = [keep.tile([P, SLOTS], U8, name=f"slot_scales{a}", align_bytes=64) for a in range(PASSES)]
+        for a in range(PASSES):
+            nc.gpsimd.memset(token_scales[a][:], 0)
 
         for a in range(PASSES):
             raw = raw_pool.tile([P, PACK, T], F32, name="raw", tag="raw")
@@ -67,17 +67,17 @@ def tile_routed_moe_kernel(tc, xT, w, gate, offs, pos1, pos2, out):
             if a == 0:
                 nc.sync.dma_start(offs_sb[:], offs)
             grouped = grouped_pool.tile([P, T, PACK], BF16, name="grouped", align_bytes=64)
-            interleave(nc.scalar.copy if a == 1 else nc.vector.tensor_copy, grouped[:], raw[:])
+            interleave(nc.vector.tensor_copy if a == 0 else nc.scalar.copy, grouped[:], raw[:])
             nc.vector.quantize_mx(
                 out=token_words[a][:].bitcast(FP8X4),
-                scales=token_scales[4 * a : P, :],
+                scales=token_scales[a][:],
                 in_=grouped[:].rearrange("p t j -> p (t j)"),
             )
         for j0, j1 in GATHER_CUTS:
-            picked = offs_sb[:, j0 // LIST_COLUMN : j1 // LIST_COLUMN]
             for a in range(PASSES):
+                picked = offs_sb[:, j0 // LIST_COLUMN : j1 // LIST_COLUMN]
                 nc.vector.tensor_copy(slot_words[a][:, j0:j1], token_words[a][:].indirect(picked))
-            nc.vector.tensor_copy(slot_scales[:, j0:j1], token_scales[:].indirect(picked))
+                nc.vector.tensor_copy(slot_scales[a][:, j0:j1], token_scales[a][:].indirect(picked))
         nc.sync.dma_start(pos1_sb[:], pos1)
         nc.sync.dma_start(pos2_sb[:], pos2)
 
@@ -86,18 +86,27 @@ def tile_routed_moe_kernel(tc, xT, w, gate, offs, pos1, pos2, out):
         gates = {}
         totals = keep.tile([P, BLOCKS, T], F32, name="totals")
 
-        def way_back(b):
-            first = stage.tile([P, T], F32, name="first")
-            second = stage.tile([P, T], F32, name="second")
-            nc.vector.tensor_tensor(first[:], y[b][:].indirect(pos1_sb[:]), gates[b][:, 0, :], MULT)
-            nc.vector.tensor_tensor(second[:], y[b][:].indirect(pos2_sb[:]), gates[b][:, 1, :], MULT)
+        def weighted(b, which, offsets):
+            part = stage.tile([P, T], F32, name=f"weighted{which}")
+            nc.vector.tensor_tensor(part[:], y[b][:].indirect(offsets[:]), gates[b][:, which, :], MULT)
+            return part
+
+        def add(b, first, second):
             nc.vector.tensor_tensor(totals[:, b, :], first[:], second[:], ADD)
+
+        def way_back(b):
+            first0 = weighted(b, 0, pos1_sb)
+            second0 = weighted(b, 1, pos2_sb)
+            first1 = weighted(b + 1, 0, pos1_sb)
+            add(b, first0, second0)
             if b == BLOCKS - 2:
                 nc.sync.dma_start(
                     out[0 : (b + 1) * P, :].rearrange("(b p) t -> p b t", p=P), totals[:, 0 : b + 1, :]
                 )
-            elif b == BLOCKS - 1:
-                nc.sync.dma_start(out[b * P : (b + 1) * P, :], totals[:, b, :])
+            second1 = weighted(b + 1, 1, pos2_sb)
+            add(b + 1, first1, second1)
+            if b == BLOCKS - 2:
+                nc.sync.dma_start(out[(b + 1) * P :, :], totals[:, b + 1, :])
 
         for step in PLAN:
             if step[0] == "gate":
@@ -138,7 +147,7 @@ def tile_routed_moe_kernel(tc, xT, w, gate, offs, pos1, pos2, out):
                         lhsT=words[a][:, cols].bitcast(FP8X4),
                         lhsT_scale=scales[a][:, cols],
                         rhs=slot_words[a][:, slots].bitcast(FP8X4),
-                        rhs_scale=slot_scales[4 * a : P, slots],
+                        rhs_scale=slot_scales[a][:, slots],
                         start=(a == 0),
                         stop=(a == PASSES - 1),
                     )

from contextlib import ExitStack

import concourse.mybir as mybir

F32 = mybir.dt.float32
BF16 = mybir.dt.bfloat16
U32 = mybir.dt.uint32
U16 = mybir.dt.uint16
U8 = mybir.dt.uint8
FP8X4 = mybir.dt.float8_e4m3fn_x4
MULT = mybir.AluOpType.mult
ADD = mybir.AluOpType.add

K, T, E, C, N = 1536, 512, 8, 128, 512
SLOTS = E * C
FLOPS = 2 * K * SLOTS * N

P = 128
PACK = 4
K_PASS = P * PACK
PASSES = K // K_PASS
BLOCKS = N // P
BANK = 512
LIST_COLUMN = 16
GATHER_CUTS = ((0, 384), (384, 768), (768, 1024))

PLAN = (
    [(e, 0, 512) for e in range(4)]
    + [(e, 0, 256) for e in range(4, 8)]
    + [("gate", 0), ("gate", 1), ("back", 0)]
    + [(e, 256, 256) for e in range(4, 8)]
    + [("gate", 2), ("gate", 3), ("back", 2)]
)

def interleave(copy, dst, src):
    copy(
        out=dst.rearrange("p (c i) t -> p c t i", i=4),
        in_=src.rearrange("p t (c i) -> p c t i", i=4),
    )


def tile_routed_moe_kernel(tc, xT, w, gate, offs, pos1, pos2, out):
    nc = tc.nc
    with ExitStack() as ctx:
        lists = ctx.enter_context(tc.tile_pool(name="lists", bufs=1))
        keep = ctx.enter_context(tc.tile_pool(name="keep", bufs=1))
        raw_pool = ctx.enter_context(tc.tile_pool(name="raw", bufs=13))
        grouped_pool = ctx.enter_context(tc.tile_pool(name="grouped", bufs=8))
        code_pool = ctx.enter_context(tc.tile_pool(name="codes", bufs=9))
        stage = ctx.enter_context(tc.tile_pool(name="stage", bufs=2))
        psum = ctx.enter_context(tc.psum_pool(name="psum", bufs=1))

        offs_sb = lists.tile([P, SLOTS // LIST_COLUMN], U16, name="offs_sb")
        pos1_sb = lists.tile([P, T // LIST_COLUMN], U16, name="pos1_sb")
        pos2_sb = lists.tile([P, T // LIST_COLUMN], U16, name="pos2_sb")

        token_words = [keep.tile([P, T], U32, name=f"token_words{a}", align_bytes=64) for a in range(PASSES)]
        token_scales = [keep.tile([P, T], U8, name=f"token_scales{a}", align_bytes=64) for a in range(PASSES)]
        slot_words = [keep.tile([P, SLOTS], U32, name=f"slot_words{a}", align_bytes=64) for a in range(PASSES)]
        slot_scales = [keep.tile([P, SLOTS], U8, name=f"slot_scales{a}", align_bytes=64) for a in range(PASSES)]
        for a in range(PASSES):
            nc.gpsimd.memset(token_scales[a][:], 0)

        for a in range(PASSES):
            raw = raw_pool.tile([P, PACK, T], F32, name="raw", tag="raw")
            nc.sync.dma_start(raw[:], xT[a * K_PASS : (a + 1) * K_PASS, :].rearrange("(p j) t -> p j t", j=PACK))
            if a == 0:
                nc.sync.dma_start(offs_sb[:], offs)
            grouped = grouped_pool.tile([P, T, PACK], BF16, name="grouped", align_bytes=64)
            interleave(nc.vector.tensor_copy if a == 0 else nc.scalar.copy, grouped[:], raw[:])
            nc.vector.quantize_mx(
                out=token_words[a][:].bitcast(FP8X4),
                scales=token_scales[a][:],
                in_=grouped[:].rearrange("p t j -> p (t j)"),
            )
        for j0, j1 in GATHER_CUTS:
            for a in range(PASSES):
                picked = offs_sb[:, j0 // LIST_COLUMN : j1 // LIST_COLUMN]
                nc.vector.tensor_copy(slot_words[a][:, j0:j1], token_words[a][:].indirect(picked))
                nc.vector.tensor_copy(slot_scales[a][:, j0:j1], token_scales[a][:].indirect(picked))
        nc.sync.dma_start(pos1_sb[:], pos1)
        nc.sync.dma_start(pos2_sb[:], pos2)

        sums = [[psum.tile([P, BANK], F32, name=f"sums{b}_{h}") for h in range(2)] for b in range(BLOCKS)]
        y = [keep.tile([P, SLOTS], F32, name=f"y{b}") for b in range(BLOCKS)]
        gates = {}
        totals = keep.tile([P, BLOCKS, T], F32, name="totals")

        def weighted(b, which, offsets):
            part = stage.tile([P, T], F32, name=f"weighted{which}")
            nc.vector.tensor_tensor(part[:], y[b][:].indirect(offsets[:]), gates[b][:, which, :], MULT)
            return part

        def add(b, first, second):
            nc.vector.tensor_tensor(totals[:, b, :], first[:], second[:], ADD)

        def way_back(b):
            first0 = weighted(b, 0, pos1_sb)
            second0 = weighted(b, 1, pos2_sb)
            first1 = weighted(b + 1, 0, pos1_sb)
            add(b, first0, second0)
            if b == BLOCKS - 2:
                nc.sync.dma_start(
                    out[0 : (b + 1) * P, :].rearrange("(b p) t -> p b t", p=P), totals[:, 0 : b + 1, :]
                )
            second1 = weighted(b + 1, 1, pos2_sb)
            add(b + 1, first1, second1)
            if b == BLOCKS - 2:
                nc.sync.dma_start(out[(b + 1) * P :, :], totals[:, b + 1, :])

        for step in PLAN:
            if step[0] == "gate":
                b = step[1]
                gates[b] = raw_pool.tile([P, 2, T], F32, name="gates", tag="raw")
                nc.sync.dma_start(gates[b][:], gate[:, b * P : (b + 1) * P, :].rearrange("g p t -> p g t"))
                continue
            if step[0] == "back":
                way_back(step[1])
                continue
            e, n0, width = step
            words = []
            scales = []
            for a in range(PASSES):
                raw = raw_pool.tile([P, PACK, width], F32, name="raw", tag="raw")
                nc.sync.dma_start(
                    raw[:],
                    w[e, a * K_PASS : (a + 1) * K_PASS, n0 : n0 + width].rearrange("(p j) n -> p j n", j=PACK),
                )
                grouped = grouped_pool.tile([P, width, PACK], BF16, name="grouped", align_bytes=64)
                interleave(nc.vector.tensor_copy if a == PASSES - 1 else nc.scalar.copy, grouped[:], raw[:])
                w_words = code_pool.tile([P, width], U32, name="w_words", align_bytes=64)
                w_scales = code_pool.tile([P, width], U8, name="w_scales", align_bytes=64)
                nc.vector.quantize_mx(
                    out=w_words[:].bitcast(FP8X4),
                    scales=w_scales[:],
                    in_=grouped[:].rearrange("p n j -> p (n j)"),
                )
                words.append(w_words)
                scales.append(w_scales)
            slots = slice(e * C, (e + 1) * C)
            bank_slots = slice(e % 4 * C, (e % 4 + 1) * C)
            for b in range(n0 // P, (n0 + width) // P):
                cols = slice(b * P - n0, (b + 1) * P - n0)
                for a in range(PASSES):
                    nc.tensor.matmul_mx(
                        out=sums[b][e // 4][:, bank_slots],
                        lhsT=words[a][:, cols].bitcast(FP8X4),
                        lhsT_scale=scales[a][:, cols],
                        rhs=slot_words[a][:, slots].bitcast(FP8X4),
                        rhs_scale=slot_scales[a][:, slots],
                        start=(a == 0),
                        stop=(a == PASSES - 1),
                    )
                if e == 3:
                    nc.scalar.copy(out=y[b][:, 0:512], in_=sums[b][0][:])
                elif e == 6:
                    nc.scalar.copy(out=y[b][:, 512:896], in_=sums[b][1][:, 0:384])
                elif e == 7:
                    nc.scalar.copy(out=y[b][:, 896:1024], in_=sums[b][1][:, 384:512])
